import numpy as np, ml_dtypes
CORES = [73,201,329,457,330]
N = 5
KT, HT, TK = 2, 2, 64
def setup_inputs(rng):
    w = (rng.standard_normal((128, KT * HT * 128), dtype=np.float32) / 8).astype(ml_dtypes.bfloat16)
    return {"x": rng.standard_normal((N, 128, KT * TK), dtype=np.float32).astype(ml_dtypes.bfloat16), "w": np.broadcast_to(w, (N,) + w.shape).copy()}
def setup_inputs_big(rng):
    d = setup_inputs(rng)
    for k in ("x", "w"): d[k] = (d[k].astype(np.float32) * 1024.0).astype(d[k].dtype)
    return d
def setup_inputs_small(rng):
    d = setup_inputs(rng)
    for k in ("x", "w"): d[k] = (d[k].astype(np.float32) * (1 / 1024.0)).astype(d[k].dtype)
    return d
def setup_inputs_apart(rng):
    d = setup_inputs(rng)
    f = (10.0 ** rng.permutation(np.linspace(-1.5, 1.5, N))).astype(np.float32).reshape(N, 1, 1)
    for k in ("x",): d[k] = (d[k].astype(np.float32) * f).astype(d[k].dtype)
    return d
def reference(x, w):
    X, W = x.astype(np.float64), w.astype(np.float64)
    def hidden(r):
        return np.stack([np.maximum(sum(W[r][:, 128 * (HT * t + u):128 * (HT * t + u) + 128].T @ X[r][:, TK * t:TK * t + TK] for t in range(KT)), 0.0) for u in range(HT)])
    h = [hidden(r) for r in range(N)]
    y = np.stack([sum(h[(r - 1) % N][u].T @ h[r][u] for u in range(HT)) for r in range(N)])
    return {"y": y.astype(ml_dtypes.bfloat16)}

@@ -1,0 +1,120 @@
+from concourse.mybir import AluOpType
+
+KT, HT, TK = 2, 2, 64
+FIRST_LEG_ENGINES = 4
+
+SCRATCH = {
+    "xd": ("dram", [128, KT * TK], "bfloat16"),
+    "hop": ("dram", [128, KT * TK], "bfloat16"),
+    "xs": ("sbuf", [128, KT * TK], "bfloat16"),
+    "ws": ("sbuf", [128, KT * HT * 128], "bfloat16"),
+    "xp": ("sbuf", [128, KT * TK], "bfloat16"),
+    "hs": ("sbuf", [128, HT * TK], "bfloat16"),
+    "hp": ("sbuf", [128, HT * TK], "bfloat16"),
+    "zero": ("sbuf", [128, TK], "float32"),
+    "ys": ("sbuf", [128, TK], "bfloat16"),
+    "ph": ("psum", [128, 512], "float32"),
+    "pp0": ("psum", [128, 512], "float32"),
+    "pp1": ("psum", [128, 512], "float32"),
+    "py": ("psum", [128, 512], "float32"),
+}
+SEMAPHORES = ["xd_in", "xs_in", "w_in", "zeroed", "own_mm", "own_h0", "own_h1", "arrived", "hop_in", "sent",
+              "p_mm0", "p_mm1", "p_h0", "p_h1", "y_mm", "y_sb", "stored"]
+
+
+def _some_engines(mask, k):
+    bits = [b for b in range(mask.bit_length()) if (mask >> b) & 1]
+    return sum(1 << b for b in bits[:k]), min(k, len(bits))
+
+
+def _ways(T, topo):
+    cores = list(T.cores)
+    ways = []
+    for r, src in enumerate(cores):
+        dst = cores[(r + 1) % len(cores)]
+        if topo.may_write(src, dst):
+            ways.append((src, None, dst))
+            continue
+        via = [m for m in cores if m not in (src, dst) and topo.may_write(src, m) and topo.may_write(m, dst)]
+        via.sort(key=lambda m: topo.same_plane(src, m))
+        ways.append((src, via[0], dst))
+    return ways
+
+
+def rank_program(g, core, T, topo):
+    rank = T.rank_of(core)
+    if rank is None:
+        return
+    S = T.sem
+    ways = _ways(T, topo)
+
+    def w_tile(t, u):
+        k = HT * t + u
+        return T.ws[:, 128 * k:128 * k + 128]
+
+    def tile(buf, j):
+        return buf[:, TK * j:TK * j + TK]
+
+    def send(dst, out, in_, sem, engines):
+        rid, pid = topo.addr(dst, core)
+        mask, n = _some_engines(topo.mask(core, dst), engines)
+        g.remote_dma(out_ap=out, in_ap=in_, remote_sem=sem, local_sem=S.sent, pid=pid, routing_id=rid,
+                     dma_engine_mask=mask)
+        return n
+
+    def engines_of(src, dst, engines):
+        return _some_engines(topo.mask(src, dst), engines)[1]
+
+    g.sync.dma_start(T.xd[:], T.x[:]).then_inc(S.xd_in, 16)
+    g.sync.dma_start(T.xs[:], T.x[:]).then_inc(S.xs_in, 16)
+    g.sync.dma_start(T.ws[:], T.w[:]).then_inc(S.w_in, 16)
+    g.vector.memset(T.zero[:], 0.0).then_inc(S.zeroed, 1)
+
+    left = 0
+    _, via, dst = ways[rank]
+    g.wait_ge(S.xd_in, 16)
+    if via is None:
+        left += send(dst, T.xp[:], T.xd[:], S.arrived, 16)
+    else:
+        left += send(via, T.hop[:], T.xd[:], S.hop_in, FIRST_LEG_ENGINES)
+    for src2, via2, dst2 in ways:
+        if via2 == core:
+            g.wait_ge(S.hop_in, engines_of(src2, core, FIRST_LEG_ENGINES))
+            left += send(dst2, T.xp[:], T.hop[:], S.arrived, 16)
+    g.wait_ge(S.sent, left)
+
+    psrc, pvia, _ = ways[(rank - 1) % len(ways)]
+    landed = engines_of(psrc if pvia is None else pvia, core, 16)
+
+    g.tensor.wait_ge(S.xs_in, 16)
+    g.tensor.wait_ge(S.w_in, 16)
+    for u in range(HT):
+        for t in range(KT):
+            mm = g.tensor.matmul(tile(T.ph, u), w_tile(t, u), tile(T.xs, t), start=(t == 0), stop=(t == KT - 1))
+    mm.then_inc(S.own_mm, 1)
+    g.vector.wait_ge(S.zeroed, 1)
+    g.vector.wait_ge(S.own_mm, 1)
+    g.vector.tensor_tensor(tile(T.hs, 0), tile(T.ph, 0), T.zero[:], AluOpType.max).then_inc(S.own_h0, 1)
+    g.vector.tensor_tensor(tile(T.hs, 1), tile(T.ph, 1), T.zero[:], AluOpType.max).then_inc(S.own_h1, 1)
+
+    banks, mm_done, h_done = (T.pp0, T.pp1), (S.p_mm0, S.p_mm1), (S.p_h0, S.p_h1)
+    g.tensor.wait_ge(S.arrived, landed)
+    for u in range(HT):
+        for t in range(KT):
+            mm = g.tensor.matmul(banks[u][:, 0:TK], w_tile(t, u), tile(T.xp, t), start=(t == 0), stop=(t == KT - 1))
+        mm.then_inc(mm_done[u], 1)
+    for u in range(HT):
+        g.vector.wait_ge(mm_done[u], 1)
+        g.vector.tensor_tensor(tile(T.hp, u), banks[u][:, 0:TK], T.zero[:], AluOpType.max).then_inc(h_done[u], 1)
+
+    own_done = (S.own_h0, S.own_h1)
+    for u in range(HT):
+        g.tensor.wait_ge(own_done[u], 1)
+        g.tensor.wait_ge(h_done[u], 1)
+        mm = g.tensor.matmul(T.py[0:TK, 0:TK], tile(T.hp, u), tile(T.hs, u), start=(u == 0), stop=(u == HT - 1))
+    mm.then_inc(S.y_mm, 1)
+    g.vector.wait_ge(S.y_mm, 1)
+    g.vector.tensor_copy(T.ys[0:TK, :], T.py[0:TK, 0:TK]).then_inc(S.y_sb, 1)
+    g.scalar.wait_ge(S.y_sb, 1)
+    g.scalar.dma_start(T.y[:], T.ys[0:TK, :]).then_inc(S.stored, 16)
+    g.scalar.wait_ge(S.stored, 16)

@@ -1,11 +1,12 @@
+from concourse.bass import DstId, RemoteDMATransfer
 from concourse.mybir import AluOpType
 
 KT, HT, TK = 2, 2, 64
-FIRST_LEG_ENGINES = 4
 
 SCRATCH = {
     "xd": ("dram", [128, KT * TK], "bfloat16"),
-    "hop": ("dram", [128, KT * TK], "bfloat16"),
+    "xc": ("dram", [KT * 128, TK], "bfloat16"),
+    "hop": ("dram", [128, TK], "bfloat16"),
     "xs": ("sbuf", [128, KT * TK], "bfloat16"),
     "ws": ("sbuf", [128, KT * HT * 128], "bfloat16"),
     "xp": ("sbuf", [128, KT * TK], "bfloat16"),
@@ -18,13 +19,14 @@ SCRATCH = {
     "pp1": ("psum", [128, 512], "float32"),
     "py": ("psum", [128, 512], "float32"),
 }
-SEMAPHORES = ["xd_in", "xs_in", "w_in", "zeroed", "own_mm", "own_h0", "own_h1", "arrived", "hop_in", "sent",
+SEMAPHORES = ["xd_in", "xs_in", "w_in", "zeroed", "own_mm", "own_h0", "own_h1", "arrived0", "arrived1", "hop_in", "sent",
               "p_mm0", "p_mm1", "p_h0", "p_h1", "y_mm", "y_sb", "stored"]
 
 
-def _some_engines(mask, k):
-    bits = [b for b in range(mask.bit_length()) if (mask >> b) & 1]
-    return sum(1 << b for b in bits[:k]), min(k, len(bits))
+def _engines(topo, src, dst, part=0, parts=1):
+    mask = topo.mask(src, dst)
+    bits = [b for b in range(mask.bit_length()) if (mask >> b) & 1][part::parts]
+    return sum(1 << b for b in bits), len(bits)
 
 
 def _ways(T, topo):
@@ -32,12 +34,12 @@ def _ways(T, topo):
     ways = []
     for r, src in enumerate(cores):
         dst = cores[(r + 1) % len(cores)]
-        if topo.may_write(src, dst):
-            ways.append((src, None, dst))
-            continue
-        via = [m for m in cores if m not in (src, dst) and topo.may_write(src, m) and topo.may_write(m, dst)]
-        via.sort(key=lambda m: topo.same_plane(src, m))
-        ways.append((src, via[0], dst))
+        via = []
+        if not topo.may_write(src, dst):
+            via = [m for m in cores if m not in (src, dst) and topo.may_write(src, m) and topo.may_write(m, dst)]
+            via.sort(key=lambda m: topo.same_plane(src, m))
+            via = [via[c % len(via)] for c in range(KT)]
+        ways.append((src, via, dst))
     return ways
 
 
@@ -47,6 +49,9 @@ def rank_program(g, core, T, topo):
         return
     S = T.sem
     ways = _ways(T, topo)
+    _, via, dst = ways[rank]
+    psrc, pvia, _ = ways[(rank - 1) % len(ways)]
+    arrived = (S.arrived0, S.arrived1)
 
     def w_tile(t, u):
         k = HT * t + u
@@ -55,39 +60,53 @@ def rank_program(g, core, T, topo):
     def tile(buf, j):
         return buf[:, TK * j:TK * j + TK]
 
-    def send(dst, out, in_, sem, engines):
-        rid, pid = topo.addr(dst, core)
-        mask, n = _some_engines(topo.mask(core, dst), engines)
+    def send(to, out, in_, sem):
+        rid, pid = topo.addr(to, core)
+        mask, n = _engines(topo, core, to)
         g.remote_dma(out_ap=out, in_ap=in_, remote_sem=sem, local_sem=S.sent, pid=pid, routing_id=rid,
                      dma_engine_mask=mask)
         return n
 
-    def engines_of(src, dst, engines):
-        return _some_engines(topo.mask(src, dst), engines)[1]
-
-    g.sync.dma_start(T.xd[:], T.x[:]).then_inc(S.xd_in, 16)
-    g.sync.dma_start(T.xs[:], T.x[:]).then_inc(S.xs_in, 16)
-    g.sync.dma_start(T.ws[:], T.w[:]).then_inc(S.w_in, 16)
+    g.sync.dma_start(T.xc[:] if via else T.xd[:], T.x[:]).then_inc(S.xd_in, 16)
+    if pvia:
+        for c in range(KT):
+            g.sync.dma_start(tile(T.xs, c), T.x[64 * c:64 * c + 64, :]).then_inc(S.xs_in, 16)
+        for c in range(KT):
+            g.sync.dma_start(T.ws[:, 128 * HT * c:128 * HT * (c + 1)], T.w[64 * c:64 * c + 64, :]).then_inc(S.w_in, 16)
+        loads = 16 * KT
+    else:
+        g.sync.dma_start(T.xs[:], T.x[:]).then_inc(S.xs_in, 16)
+        g.sync.dma_start(T.ws[:], T.w[:]).then_inc(S.w_in, 16)
+        loads = 16
     g.vector.memset(T.zero[:], 0.0).then_inc(S.zeroed, 1)
 
     left = 0
-    _, via, dst = ways[rank]
     g.wait_ge(S.xd_in, 16)
-    if via is None:
-        left += send(dst, T.xp[:], T.xd[:], S.arrived, 16)
+    if not via:
+        left += send(dst, T.xp[:], T.xd[:], S.arrived0)
     else:
-        left += send(via, T.hop[:], T.xd[:], S.hop_in, FIRST_LEG_ENGINES)
+        transfers = []
+        for c, m in enumerate(via):
+            rid, pid = topo.addr(m, core)
+            mask, n = _engines(topo, core, m, c, len(via))
+            transfers.append(RemoteDMATransfer(dst_ids=[DstId(rid=rid, pnc=pid)], dma_engine_mask=mask,
+                                               remote_sem=S.hop_in, src=T.xc[128 * c:128 * c + 128, :], dst=T.hop[:]))
+            left += n
+        g.remote_dma_fused(transfers, local_sem=S.sent)
     for src2, via2, dst2 in ways:
-        if via2 == core:
-            g.wait_ge(S.hop_in, engines_of(src2, core, FIRST_LEG_ENGINES))
-            left += send(dst2, T.xp[:], T.hop[:], S.arrived, 16)
+        for c, m in enumerate(via2):
+            if m == core:
+                g.wait_ge(S.hop_in, _engines(topo, src2, core, c, len(via2))[1])
+                left += send(dst2, tile(T.xp, c), T.hop[:], arrived[c])
     g.wait_ge(S.sent, left)
 
-    psrc, pvia, _ = ways[(rank - 1) % len(ways)]
-    landed = engines_of(psrc if pvia is None else pvia, core, 16)
+    if pvia:
+        landed = [(arrived[c], _engines(topo, m, core)[1]) for c, m in enumerate(pvia)]
+    else:
+        landed = [(arrived[0], _engines(topo, psrc, core)[1])] + [None] * (KT - 1)
 
-    g.tensor.wait_ge(S.xs_in, 16)
-    g.tensor.wait_ge(S.w_in, 16)
+    g.tensor.wait_ge(S.xs_in, loads)
+    g.tensor.wait_ge(S.w_in, loads)
     for u in range(HT):
         for t in range(KT):
             mm = g.tensor.matmul(tile(T.ph, u), w_tile(t, u), tile(T.xs, t), start=(t == 0), stop=(t == KT - 1))
@@ -98,11 +117,13 @@ def rank_program(g, core, T, topo):
     g.vector.tensor_tensor(tile(T.hs, 1), tile(T.ph, 1), T.zero[:], AluOpType.max).then_inc(S.own_h1, 1)
 
     banks, mm_done, h_done = (T.pp0, T.pp1), (S.p_mm0, S.p_mm1), (S.p_h0, S.p_h1)
-    g.tensor.wait_ge(S.arrived, landed)
-    for u in range(HT):
-        for t in range(KT):
+    for t in range(KT):
+        if landed[t] is not None:
+            g.tensor.wait_ge(landed[t][0], landed[t][1])
+        for u in range(HT):
             mm = g.tensor.matmul(banks[u][:, 0:TK], w_tile(t, u), tile(T.xp, t), start=(t == 0), stop=(t == KT - 1))
-        mm.then_inc(mm_done[u], 1)
+            if t == KT - 1:
+                mm.then_inc(mm_done[u], 1)
     for u in range(HT):
         g.vector.wait_ge(mm_done[u], 1)
         g.vector.tensor_tensor(tile(T.hp, u), banks[u][:, 0:TK], T.zero[:], AluOpType.max).then_inc(h_done[u], 1)

from concourse.bass import DstId, RemoteDMATransfer
from concourse.mybir import AluOpType

KT, HT, TK = 2, 2, 64

SCRATCH = {
    "xd": ("dram", [128, KT * TK], "bfloat16"),
    "xc": ("dram", [KT * 128, TK], "bfloat16"),
    "hop": ("dram", [128, TK], "bfloat16"),
    "xs": ("sbuf", [128, KT * TK], "bfloat16"),
    "ws": ("sbuf", [128, KT * HT * 128], "bfloat16"),
    "xp": ("sbuf", [128, KT * TK], "bfloat16"),
    "hs": ("sbuf", [128, HT * TK], "bfloat16"),
    "hp": ("sbuf", [128, HT * TK], "bfloat16"),
    "zero": ("sbuf", [128, TK], "float32"),
    "ys": ("sbuf", [128, TK], "bfloat16"),
    "ph": ("psum", [128, 512], "float32"),
    "pp0": ("psum", [128, 512], "float32"),
    "pp1": ("psum", [128, 512], "float32"),
    "py": ("psum", [128, 512], "float32"),
}
SEMAPHORES = ["xd_in", "xs_in", "w_in", "zeroed", "own_mm", "own_h0", "own_h1", "arrived0", "arrived1", "hop_in", "sent",
              "p_mm0", "p_mm1", "p_h0", "p_h1", "y_mm", "y_sb", "stored"]


def _engines(topo, src, dst, part=0, parts=1):
    mask = topo.mask(src, dst)
    bits = [b for b in range(mask.bit_length()) if (mask >> b) & 1][part::parts]
    return sum(1 << b for b in bits), len(bits)


def _ways(T, topo):
    cores = list(T.cores)
    ways = []
    for r, src in enumerate(cores):
        dst = cores[(r + 1) % len(cores)]
        via = []
        if not topo.may_write(src, dst):
            via = [m for m in cores if m not in (src, dst) and topo.may_write(src, m) and topo.may_write(m, dst)]
            via.sort(key=lambda m: topo.same_plane(src, m))
            via = [via[c % len(via)] for c in range(KT)]
        ways.append((src, via, dst))
    return ways


def rank_program(g, core, T, topo):
    rank = T.rank_of(core)
    if rank is None:
        return
    S = T.sem
    ways = _ways(T, topo)
    _, via, dst = ways[rank]
    psrc, pvia, _ = ways[(rank - 1) % len(ways)]
    arrived = (S.arrived0, S.arrived1)

    def w_tile(t, u):
        k = HT * t + u
        return T.ws[:, 128 * k:128 * k + 128]

    def tile(buf, j):
        return buf[:, TK * j:TK * j + TK]

    def send(to, out, in_, sem):
        rid, pid = topo.addr(to, core)
        mask, n = _engines(topo, core, to)
        g.remote_dma(out_ap=out, in_ap=in_, remote_sem=sem, local_sem=S.sent, pid=pid, routing_id=rid,
                     dma_engine_mask=mask)
        return n

    g.sync.dma_start(T.xc[:] if via else T.xd[:], T.x[:]).then_inc(S.xd_in, 16)
    if pvia:
        for c in range(KT):
            g.sync.dma_start(tile(T.xs, c), T.x[64 * c:64 * c + 64, :]).then_inc(S.xs_in, 16)
        for c in range(KT):
            g.sync.dma_start(T.ws[:, 128 * HT * c:128 * HT * (c + 1)], T.w[64 * c:64 * c + 64, :]).then_inc(S.w_in, 16)
        loads = 16 * KT
    else:
        g.sync.dma_start(T.xs[:], T.x[:]).then_inc(S.xs_in, 16)
        g.sync.dma_start(T.ws[:], T.w[:]).then_inc(S.w_in, 16)
        loads = 16
    g.vector.memset(T.zero[:], 0.0).then_inc(S.zeroed, 1)

    left = 0
    g.wait_ge(S.xd_in, 16)
    if not via:
        left += send(dst, T.xp[:], T.xd[:], S.arrived0)
    else:
        transfers = []
        for c, m in enumerate(via):
            rid, pid = topo.addr(m, core)
            mask, n = _engines(topo, core, m, c, len(via))
            transfers.append(RemoteDMATransfer(dst_ids=[DstId(rid=rid, pnc=pid)], dma_engine_mask=mask,
                                               remote_sem=S.hop_in, src=T.xc[128 * c:128 * c + 128, :], dst=T.hop[:]))
            left += n
        g.remote_dma_fused(transfers, local_sem=S.sent)
    for src2, via2, dst2 in ways:
        for c, m in enumerate(via2):
            if m == core:
                g.wait_ge(S.hop_in, _engines(topo, src2, core, c, len(via2))[1])
                left += send(dst2, tile(T.xp, c), T.hop[:], arrived[c])
    g.wait_ge(S.sent, left)

    if pvia:
        landed = [(arrived[c], _engines(topo, m, core)[1]) for c, m in enumerate(pvia)]
    else:
        landed = [(arrived[0], _engines(topo, psrc, core)[1])] + [None] * (KT - 1)

    g.tensor.wait_ge(S.xs_in, loads)
    g.tensor.wait_ge(S.w_in, loads)
    for u in range(HT):
        for t in range(KT):
            mm = g.tensor.matmul(tile(T.ph, u), w_tile(t, u), tile(T.xs, t), start=(t == 0), stop=(t == KT - 1))
    mm.then_inc(S.own_mm, 1)
    g.vector.wait_ge(S.zeroed, 1)
    g.vector.wait_ge(S.own_mm, 1)
    g.vector.tensor_tensor(tile(T.hs, 0), tile(T.ph, 0), T.zero[:], AluOpType.max).then_inc(S.own_h0, 1)
    g.vector.tensor_tensor(tile(T.hs, 1), tile(T.ph, 1), T.zero[:], AluOpType.max).then_inc(S.own_h1, 1)

    banks, mm_done, h_done = (T.pp0, T.pp1), (S.p_mm0, S.p_mm1), (S.p_h0, S.p_h1)
    for t in range(KT):
        if landed[t] is not None:
            g.tensor.wait_ge(landed[t][0], landed[t][1])
        for u in range(HT):
            mm = g.tensor.matmul(banks[u][:, 0:TK], w_tile(t, u), tile(T.xp, t), start=(t == 0), stop=(t == KT - 1))
            if t == KT - 1:
                mm.then_inc(mm_done[u], 1)
    for u in range(HT):
        g.vector.wait_ge(mm_done[u], 1)
        g.vector.tensor_tensor(tile(T.hp, u), banks[u][:, 0:TK], T.zero[:], AluOpType.max).then_inc(h_done[u], 1)

    own_done = (S.own_h0, S.own_h1)
    for u in range(HT):
        g.tensor.wait_ge(own_done[u], 1)
        g.tensor.wait_ge(h_done[u], 1)
        mm = g.tensor.matmul(T.py[0:TK, 0:TK], tile(T.hp, u), tile(T.hs, u), start=(u == 0), stop=(u == HT - 1))
    mm.then_inc(S.y_mm, 1)
    g.vector.wait_ge(S.y_mm, 1)
    g.vector.tensor_copy(T.ys[0:TK, :], T.py[0:TK, 0:TK]).then_inc(S.y_sb, 1)
    g.scalar.wait_ge(S.y_sb, 1)
    g.scalar.dma_start(T.y[:], T.ys[0:TK, :]).then_inc(S.stored, 16)
    g.scalar.wait_ge(S.stored, 16)
